import numpy as np
import ml_dtypes


def mxq(x, axis, fmt="e4m3"):
    dtype, down = {"e4m3": (ml_dtypes.float8_e4m3fn, 7), "e5m2": (ml_dtypes.float8_e5m2, 14)}[fmt]
    v = np.moveaxis(np.asarray(x, np.float32).astype(ml_dtypes.bfloat16).astype(np.float64), axis, -1)
    blocks = v.reshape(v.shape[:-1] + (-1, 32))
    amax = np.abs(blocks).max(-1, keepdims=True)
    byte = np.maximum(np.where(amax > 0, np.frexp(amax)[1] - 1 + 127, 0) - down, 1)
    scale = np.exp2(byte - 127.0)
    codes = (blocks / scale).astype(np.float32).astype(dtype).astype(np.float64)
    return np.moveaxis((codes * scale).reshape(v.shape), -1, axis)


WIDE = False


def mx_kscale(k):
    if not WIDE:
        return np.ones(k)
    levels = np.array([10, -10, 5, -5, 0])
    if k % 512:
        return np.exp2(np.random.permutation(np.resize(levels, k // 32))).repeat(32)
    a = np.empty((k // 512, 16))
    for p in range(k // 512):
        a[p, :8] = np.random.permutation(np.resize(levels, 8))
        for g in range(8):
            far = levels[np.abs(levels - a[p, g]) >= 10]
            a[p, g + 8] = far[np.random.randint(len(far))]
    return np.exp2(a.ravel()).repeat(32)


def f64(x):
    return np.asarray(x).astype(np.float64)


def striped(idx):
    return np.tile(idx.reshape(-1, 16).T, (8, 1)).astype(np.uint16)


def unstriped(offs):
    return offs[:16].T.reshape(-1).astype(np.int64)


def striped8(idx):
    return np.concatenate([x.reshape(-1, 16).T for x in idx]).astype(np.uint16)


def runs(offs, k):
    lists = np.stack([offs[16 * r : 16 * r + 16].T.reshape(-1) for r in range(8)]).astype(np.int64)
    return lists[np.arange(k) % 512 // 64]


def pack_weight(w):
    k, n = w.shape
    w = f64(np.asarray(w, np.float32).astype(ml_dtypes.bfloat16)).reshape(k // 32, 32, n)
    amax = np.abs(w).max(1)
    byte = np.clip(np.where(amax > 0, np.frexp(amax)[1] - 1 + 127 - 7, 1), 1, 254)
    scaled = (w * np.exp2(127.0 - byte)[:, None, :]).reshape(k, n).astype(np.float32)
    words = np.ascontiguousarray(scaled.reshape(k // 512, 128, 4, n).transpose(0, 1, 3, 2)).astype(ml_dtypes.float8_e4m3fn).view(np.uint8)
    return words, np.ascontiguousarray(byte.astype(np.uint8).reshape(k // 512, 16, n))


def unpack_weight(words, scales):
    g, p, n, _ = words.shape
    vals = np.ascontiguousarray(words).view(ml_dtypes.float8_e4m3fn).astype(np.float64) * np.repeat(np.exp2(scales.astype(np.float64) - 127.0), 8, axis=1)[..., None]
    return vals.transpose(0, 1, 3, 2).reshape(g * 512, n)


def relu(v):
    return np.maximum(v, 0.0)


K, T, S, V, H = 512, 2048, 512, 512, 512


def setup_inputs():
    n = np.random.standard_normal
    s = mx_kscale(K)[:, None]
    packed_xT = pack_weight(n((K, T)) * s)
    return {
        "x_words": packed_xT[0],
        "x_scales": packed_xT[1],
        "w1": (n((K, H)) / np.sqrt(K) / s).astype(np.float32),
        "gs": (np.random.uniform(0.5, 1.5, (K, 1)) / s).astype(np.float32),
        "offs": striped(np.random.permutation(T)[:S]),
        "cand": striped(np.random.permutation(T)[:V]),
        "neg": striped8(np.stack([np.random.permutation(S) for _ in range(8)])),
    }


def reference(x_words, x_scales, w1, gs, offs, cand, neg):
    x_cand = unpack_weight(x_words, x_scales)[:, unstriped(cand)]
    xq = unpack_weight(x_words, x_scales)[:, unstriped(offs)]
    h = relu(mxq(f64(w1), 0, "e4m3").T @ xq)
    z = f64(gs) * h
    s = 0.0625 * ((x_cand.T @ mxq(z, 0, "e4m3")))
    return relu(s[np.arange(V)[:, None], runs(neg, V)] - s + 1)

@@ -1,0 +1,171 @@
+from contextlib import ExitStack
+
+import concourse.mybir as mybir
+
+K, T, S, V, H = 512, 2048, 512, 512, 512
+FLOPS = 2 * K * H * S + 2 * K * V * S
+
+F32 = mybir.dt.float32
+BF16 = mybir.dt.bfloat16
+I32 = mybir.dt.int32
+U32 = mybir.dt.uint32
+U16 = mybir.dt.uint16
+U8 = mybir.dt.uint8
+FP8X4 = mybir.dt.float8_e4m3fn_x4
+ALU = mybir.AluOpType
+ACT = mybir.ActivationFunctionType
+
+P = 128
+PACK = 4
+CH = 128
+SCORE_SCALE = 0.0625
+
+
+def tile_picked_candhinge_none_p_kernel(tc, x_words, x_scales, w1, gs, offs, cand, neg, out):
+    nc = tc.nc
+    with ExitStack() as ctx:
+        lists = ctx.enter_context(tc.tile_pool(name="lists", bufs=1))
+        sb = ctx.enter_context(tc.tile_pool(name="sb", bufs=1))
+        ps = ctx.enter_context(tc.psum_pool(name="ps", bufs=1))
+
+        offs_t = lists.tile([P, S // 16], U16, name="offs_t")
+        cand_t = lists.tile([P, V // 16], U16, name="cand_t")
+        neg_t = lists.tile([P, S // 16], U16, name="neg_t")
+
+        xw = sb.tile([P, T], I32, name="xw", align_bytes=64)
+        xs = sb.tile([P, T], U8, name="xs", align_bytes=64)
+        gs_t = sb.tile([P, PACK], F32, name="gs_t")
+        w_raw = [sb.tile([P, PACK, CH], F32, name="w_raw%d" % c, align_bytes=64) for c in range(4)]
+        w_view = w1.rearrange("(p j) c -> p j c", j=PACK)
+
+        nc.vector.memset(xs[:].bitcast(I32), 0)
+        nc.sync.dma_start(out=w_raw[0][:], in_=w_view[:, :, 0:CH])
+        nc.sync.dma_start(offs_t[:], offs)
+        nc.sync.dma_start(cand_t[:], cand)
+        for q in range(4):
+            nc.sync.dma_start(out=xs[32 * q : 32 * q + 4, :].bitcast(I32), in_=x_scales[0, 4 * q : 4 * q + 4, :].bitcast(I32))
+        nc.sync.dma_start(out=xw[:], in_=x_words[0].rearrange("p n t -> p (n t)").bitcast(I32))
+        for c in range(1, 4):
+            nc.sync.dma_start(out=w_raw[c][:], in_=w_view[:, :, c * CH : (c + 1) * CH])
+        nc.sync.dma_start(out=gs_t[:], in_=gs.rearrange("(p t) o -> p (t o)", t=PACK))
+        nc.sync.dma_start(neg_t[:], neg)
+
+        tok_w = sb.tile([P, S], U32, name="tok_w", align_bytes=64)
+        tok_s = sb.tile([P, S], U8, name="tok_s", align_bytes=64)
+        cand_w = sb.tile([P, PACK, P], U32, name="cand_w", align_bytes=64)
+        cand_s = sb.tile([P, PACK, P], U8, name="cand_s", align_bytes=64)
+        nc.vector.tensor_copy(tok_s[:], xs[:].indirect(offs_t[:]))
+        nc.vector.tensor_copy(cand_s[:].rearrange("p t m -> p m t"), xs[:].indirect(cand_t[:]))
+        nc.vector.tensor_copy(tok_w[:], xw[:].bitcast(U32).indirect(offs_t[:]))
+        nc.vector.tensor_copy(cand_w[:].rearrange("p t m -> p m t"), xw[:].bitcast(U32).indirect(cand_t[:]))
+
+        w_codes = sb.tile([P, PACK, P], U32, name="w_codes", align_bytes=64)
+        w_scales = sb.tile([P, PACK, P], U8, name="w_scales", align_bytes=64)
+        for half in range(2):
+            w_bf = sb.tile([P, PACK, 64, PACK], BF16, name="w_bf%d" % half, align_bytes=64)
+            for i in range(2):
+                nc.scalar.copy(
+                    out=w_bf[:, :, 32 * i : 32 * i + 32, :].rearrange("p t m j -> p m t j"),
+                    in_=w_raw[2 * half + i][:].rearrange("p j (m t) -> p m t j", t=PACK),
+                )
+            for t in range(PACK):
+                nc.vector.quantize_mx(
+                    out=w_codes[:, t, 64 * half : 64 * half + 64].bitcast(FP8X4),
+                    scales=w_scales[:, t, 64 * half : 64 * half + 64],
+                    in_=w_bf[:, t, :, :].rearrange("p m j -> p (m j)"),
+                )
+
+        z_codes = sb.tile([P, S], U32, name="z_codes", align_bytes=64)
+        z_scales = sb.tile([P, S], U8, name="z_scales", align_bytes=64)
+        gs_b = gs_t[:].rearrange("p (o t) -> p o t", o=1).to_broadcast([P, CH, PACK])
+        z_bf = []
+        for c in range(4):
+            cols = slice(c * CH, (c + 1) * CH)
+            h_ps = ps.tile([P, PACK, CH], F32, name="h_ps%d" % c)
+            for t in range(PACK):
+                nc.tensor.matmul_mx(
+                    out=h_ps[:, t, :],
+                    lhsT=w_codes[:, t, :].bitcast(FP8X4), lhsT_scale=w_scales[:, t, :],
+                    rhs=tok_w[:, cols].bitcast(FP8X4), rhs_scale=tok_s[:, cols],
+                    start=True, stop=True,
+                )
+            zb = sb.tile([P, CH, PACK], BF16, name="z_bf%d" % c, align_bytes=64)
+            z_bf.append((zb, h_ps))
+
+        def scale_z(c):
+            zb, h_ps = z_bf[c]
+            nc.vector.scalar_tensor_tensor(
+                out=zb[:], in0=h_ps[:].rearrange("p t n -> p n t"), scalar=0.0, in1=gs_b, op0=ALU.max, op1=ALU.mult
+            )
+
+        def quant_z(c):
+            cols = slice(c * CH, (c + 1) * CH)
+            nc.vector.quantize_mx(
+                out=z_codes[:, cols].bitcast(FP8X4), scales=z_scales[:, cols], in_=z_bf[c][0][:].rearrange("p n t -> p (n t)")
+            )
+
+        s_ps = [ps.tile([P, S], F32, name="s_ps%d" % t) for t in range(PACK)]
+        win = [sb.tile([P, S], F32, name="win%d" % t, align_bytes=64) for t in range(PACK)]
+
+        def score(cols, on_vector):
+            for t in range(PACK):
+                nc.tensor.matmul_mx(
+                    out=s_ps[t][:, cols],
+                    lhsT=cand_w[:, t, :].bitcast(FP8X4), lhsT_scale=cand_s[:, t, :],
+                    rhs=z_codes[:, cols].bitcast(FP8X4), rhs_scale=z_scales[:, cols],
+                    start=True, stop=True,
+                )
+            for t in range(PACK):
+                if t in on_vector:
+                    nc.vector.tensor_scalar(win[t][:, cols], s_ps[t][:, cols], SCORE_SCALE, 1.0, op0=ALU.mult, op1=ALU.add)
+                else:
+                    nc.scalar.activation(out=win[t][:, cols], in_=s_ps[t][:, cols], func=ACT.Copy, scale=SCORE_SCALE, bias=1.0)
+
+        scale_z(0)
+        scale_z(1)
+        quant_z(0)
+        scale_z(2)
+        quant_z(1)
+        score(slice(0, 256), ())
+        scale_z(3)
+        quant_z(2)
+        score(slice(256, 384), ())
+        quant_z(3)
+        score(slice(384, 512), (1, 2, 3))
+
+        out_v = out.rearrange("(p t) c -> t p c", t=PACK)
+        units = [(t, u) for t in range(PACK) for u in range(2)]
+        got = {}
+
+        def fetch(t, u, on_vector):
+            g = sb.tile([P, 256], F32, name="got%d_%d" % (t, u), align_bytes=64)
+            got[(t, u)] = g
+            src = win[t][:].indirect(neg_t[:, 16 * u : 16 * u + 16])
+            if on_vector:
+                nc.vector.tensor_copy(g[:], src)
+            else:
+                nc.scalar.activation(out=g[:], in_=src, func=ACT.Copy)
+
+        diff = {}
+
+        def subtract(t, u):
+            d = sb.tile([P, 256], F32, name="diff%d_%d" % (t, u), align_bytes=64)
+            diff[(t, u)] = d
+            nc.vector.scalar_tensor_tensor(
+                out=d[:], in0=s_ps[t][:, 256 * u : 256 * u + 256], scalar=-SCORE_SCALE, in1=got[(t, u)][:], op0=ALU.mult, op1=ALU.add
+            )
+
+        def finish(t, u):
+            r = sb.tile([P, 256], F32, name="res%d_%d" % (t, u), align_bytes=64)
+            nc.vector.tensor_scalar(r[:], diff[(t, u)][:], 0.0, None, op0=ALU.max)
+            nc.sync.dma_start(out=out_v[t, :, 256 * u : 256 * u + 256], in_=r[:])
+
+        order = [(3, 1)] + units[:-1]
+        fetch(3, 1, True)
+        for t, u in units[:-1]:
+            fetch(t, u, False)
+        for i, (t, u) in enumerate(order):
+            subtract(t, u)
+            if i > 0:
+                finish(*order[i - 1])
+        finish(*order[-1])

@@ -35,19 +35,24 @@ def tile_picked_candhinge_none_p_kernel(tc, x_words, x_scales, w1, gs, offs, can
         xw = sb.tile([P, T], I32, name="xw", align_bytes=64)
         xs = sb.tile([P, T], U8, name="xs", align_bytes=64)
         gs_t = sb.tile([P, PACK], F32, name="gs_t")
-        w_raw = [sb.tile([P, PACK, CH], F32, name="w_raw%d" % c, align_bytes=64) for c in range(4)]
         w_view = w1.rearrange("(p j) c -> p j c", j=PACK)
+        w_parts = [(0, 1), (1, 3), (3, 4)]
+        w_raw = [sb.tile([P, PACK, (c1 - c0) * CH], F32, name="w_raw%d" % c0, align_bytes=64) for c0, c1 in w_parts]
+
+        def load_w(i):
+            c0, c1 = w_parts[i]
+            nc.sync.dma_start(out=w_raw[i][:], in_=w_view[:, :, c0 * CH : c1 * CH])
 
         nc.vector.memset(xs[:].bitcast(I32), 0)
-        nc.sync.dma_start(out=w_raw[0][:], in_=w_view[:, :, 0:CH])
+        nc.gpsimd.dma_start(out=gs_t[:], in_=gs.rearrange("(p t) o -> p (t o)", t=PACK))
         nc.sync.dma_start(offs_t[:], offs)
         nc.sync.dma_start(cand_t[:], cand)
+        load_w(0)
         for q in range(4):
             nc.sync.dma_start(out=xs[32 * q : 32 * q + 4, :].bitcast(I32), in_=x_scales[0, 4 * q : 4 * q + 4, :].bitcast(I32))
+        load_w(1)
+        load_w(2)
         nc.sync.dma_start(out=xw[:], in_=x_words[0].rearrange("p n t -> p (n t)").bitcast(I32))
-        for c in range(1, 4):
-            nc.sync.dma_start(out=w_raw[c][:], in_=w_view[:, :, c * CH : (c + 1) * CH])
-        nc.sync.dma_start(out=gs_t[:], in_=gs.rearrange("(p t) o -> p (t o)", t=PACK))
         nc.sync.dma_start(neg_t[:], neg)
 
         tok_w = sb.tile([P, S], U32, name="tok_w", align_bytes=64)
@@ -56,17 +61,17 @@ def tile_picked_candhinge_none_p_kernel(tc, x_words, x_scales, w1, gs, offs, can
         cand_s = sb.tile([P, PACK, P], U8, name="cand_s", align_bytes=64)
         nc.vector.tensor_copy(tok_s[:], xs[:].indirect(offs_t[:]))
         nc.vector.tensor_copy(cand_s[:].rearrange("p t m -> p m t"), xs[:].indirect(cand_t[:]))
-        nc.vector.tensor_copy(tok_w[:], xw[:].bitcast(U32).indirect(offs_t[:]))
-        nc.vector.tensor_copy(cand_w[:].rearrange("p t m -> p m t"), xw[:].bitcast(U32).indirect(cand_t[:]))
 
         w_codes = sb.tile([P, PACK, P], U32, name="w_codes", align_bytes=64)
         w_scales = sb.tile([P, PACK, P], U8, name="w_scales", align_bytes=64)
         for half in range(2):
             w_bf = sb.tile([P, PACK, 64, PACK], BF16, name="w_bf%d" % half, align_bytes=64)
             for i in range(2):
-                nc.scalar.copy(
+                src = [w_raw[0][:], w_raw[1][:, :, 0:CH], w_raw[1][:, :, CH : 2 * CH], w_raw[2][:]][2 * half + i]
+                cast = nc.vector.tensor_copy if 2 * half + i == 3 else nc.scalar.copy
+                cast(
                     out=w_bf[:, :, 32 * i : 32 * i + 32, :].rearrange("p t m j -> p m t j"),
-                    in_=w_raw[2 * half + i][:].rearrange("p j (m t) -> p m t j", t=PACK),
+                    in_=src.rearrange("p j (m t) -> p m t j", t=PACK),
                 )
             for t in range(PACK):
                 nc.vector.quantize_mx(
@@ -74,6 +79,10 @@ def tile_picked_candhinge_none_p_kernel(tc, x_words, x_scales, w1, gs, offs, can
                     scales=w_scales[:, t, 64 * half : 64 * half + 64],
                     in_=w_bf[:, t, :, :].rearrange("p m j -> p (m j)"),
                 )
+
+        for a, b in ((0, 128), (128, 256), (256, 512)):
+            nc.vector.tensor_copy(tok_w[:, a:b], xw[:].bitcast(U32).indirect(offs_t[:, a // 16 : b // 16]))
+        nc.vector.tensor_copy(cand_w[:].rearrange("p t m -> p m t"), xw[:].bitcast(U32).indirect(cand_t[:]))
 
         z_codes = sb.tile([P, S], U32, name="z_codes", align_bytes=64)
         z_scales = sb.tile([P, S], U8, name="z_scales", align_bytes=64)
@@ -104,38 +113,49 @@ def tile_picked_candhinge_none_p_kernel(tc, x_words, x_scales, w1, gs, offs, can
                 out=z_codes[:, cols].bitcast(FP8X4), scales=z_scales[:, cols], in_=z_bf[c][0][:].rearrange("p n t -> p (n t)")
             )
 
-        s_ps = [ps.tile([P, S], F32, name="s_ps%d" % t) for t in range(PACK)]
+        def scale_z_aside(c):
+            zb, h_ps = z_bf[c]
+            pos = sb.tile([P, CH, PACK], F32, name="pos%d" % c, align_bytes=64)
+            nc.scalar.activation(out=pos[:], in_=h_ps[:].rearrange("p t n -> p n t"), func=ACT.Relu)
+            nc.gpsimd.tensor_tensor(out=zb[:], in0=pos[:], in1=gs_b, op=ALU.mult)
+
+        s_ps = [[ps.tile([P, 2, 256], F32, name="s_ps%d_%d" % (u, g)) for g in range(2)] for u in range(2)]
         win = [sb.tile([P, S], F32, name="win%d" % t, align_bytes=64) for t in range(PACK)]
 
-        def score(cols, on_vector):
-            for t in range(PACK):
+        def score(a, b, order):
+            for t in order:
                 nc.tensor.matmul_mx(
-                    out=s_ps[t][:, cols],
+                    out=s_ps[a // 256][t // 2][:, t % 2, a % 256 : a % 256 + b - a],
                     lhsT=cand_w[:, t, :].bitcast(FP8X4), lhsT_scale=cand_s[:, t, :],
-                    rhs=z_codes[:, cols].bitcast(FP8X4), rhs_scale=z_scales[:, cols],
+                    rhs=z_codes[:, a:b].bitcast(FP8X4), rhs_scale=z_scales[:, a:b],
                     start=True, stop=True,
                 )
-            for t in range(PACK):
-                if t in on_vector:
-                    nc.vector.tensor_scalar(win[t][:, cols], s_ps[t][:, cols], SCORE_SCALE, 1.0, op0=ALU.mult, op1=ALU.add)
-                else:
-                    nc.scalar.activation(out=win[t][:, cols], in_=s_ps[t][:, cols], func=ACT.Copy, scale=SCORE_SCALE, bias=1.0)
 
-        scale_z(0)
+        def to_window(t, u, on_vector):
+            dst = win[t][:, 256 * u : 256 * u + 256]
+            src = s_ps[u][t // 2][:, t % 2, :]
+            if on_vector:
+                nc.vector.tensor_scalar(dst, src, SCORE_SCALE, 1.0, op0=ALU.mult, op1=ALU.add)
+            else:
+                nc.scalar.activation(out=dst, in_=src, func=ACT.Copy, scale=SCORE_SCALE, bias=1.0)
+
+        scale_z_aside(0)
         scale_z(1)
-        quant_z(0)
         scale_z(2)
         quant_z(1)
-        score(slice(0, 256), ())
+        quant_z(0)
+        score(0, 256, range(PACK))
+        for t in range(PACK):
+            to_window(t, 0, False)
         scale_z(3)
         quant_z(2)
-        score(slice(256, 384), ())
+        score(256, 384, range(PACK))
         quant_z(3)
-        score(slice(384, 512), (1, 2, 3))
+        score(384, 512, range(PACK))
 
         out_v = out.rearrange("(p t) c -> t p c", t=PACK)
-        units = [(t, u) for t in range(PACK) for u in range(2)]
         got = {}
+        diff = {}
 
         def fetch(t, u, on_vector):
             g = sb.tile([P, 256], F32, name="got%d_%d" % (t, u), align_bytes=64)
@@ -146,26 +166,47 @@ def tile_picked_candhinge_none_p_kernel(tc, x_words, x_scales, w1, gs, offs, can
             else:
                 nc.scalar.activation(out=g[:], in_=src, func=ACT.Copy)
 
-        diff = {}
-
         def subtract(t, u):
             d = sb.tile([P, 256], F32, name="diff%d_%d" % (t, u), align_bytes=64)
-            diff[(t, u)] = d
             nc.vector.scalar_tensor_tensor(
-                out=d[:], in0=s_ps[t][:, 256 * u : 256 * u + 256], scalar=-SCORE_SCALE, in1=got[(t, u)][:], op0=ALU.mult, op1=ALU.add
+                out=d[:], in0=s_ps[u][t // 2][:, t % 2, :], scalar=-SCORE_SCALE, in1=got[(t, u)][:], op0=ALU.mult, op1=ALU.add
             )
+            diff[(t, u)] = d
 
-        def finish(t, u):
+        def finish(t, u, on_vector):
+            d = diff[(t, u)]
             r = sb.tile([P, 256], F32, name="res%d_%d" % (t, u), align_bytes=64)
-            nc.vector.tensor_scalar(r[:], diff[(t, u)][:], 0.0, None, op0=ALU.max)
+            if not on_vector:
+                nc.scalar.activation(out=r[:], in_=d[:], func=ACT.Relu)
+            else:
+                nc.vector.tensor_scalar(r[:], d[:], 0.0, None, op0=ALU.max)
             nc.sync.dma_start(out=out_v[t, :, 256 * u : 256 * u + 256], in_=r[:])
 
-        order = [(3, 1)] + units[:-1]
+        to_window(0, 1, False)
+        to_window(3, 1, True)
+        to_window(2, 1, True)
+        fetch(0, 0, False)
+        fetch(3, 0, True)
+        fetch(0, 1, False)
+        to_window(1, 1, False)
+        subtract(0, 0)
+        subtract(3, 0)
+        finish(0, 0, True)
         fetch(3, 1, True)
-        for t, u in units[:-1]:
-            fetch(t, u, False)
-        for i, (t, u) in enumerate(order):
-            subtract(t, u)
-            if i > 0:
-                finish(*order[i - 1])
-        finish(*order[-1])
+        finish(3, 0, True)
+        fetch(1, 0, False)
+        fetch(1, 1, False)
+        fetch(2, 0, False)
+        fetch(2, 1, False)
+        subtract(0, 1)
+        subtract(3, 1)
+        finish(0, 1, True)
+        subtract(1, 0)
+        finish(3, 1, True)
+        subtract(1, 1)
+        finish(1, 0, True)
+        subtract(2, 0)
+        finish(1, 1, False)
+        subtract(2, 1)
+        finish(2, 0, False)
+        finish(2, 1, True)

from contextlib import ExitStack

import concourse.mybir as mybir

K, T, S, V, H = 512, 2048, 512, 512, 512
FLOPS = 2 * K * H * S + 2 * K * V * S

F32 = mybir.dt.float32
BF16 = mybir.dt.bfloat16
I32 = mybir.dt.int32
U32 = mybir.dt.uint32
U16 = mybir.dt.uint16
U8 = mybir.dt.uint8
FP8X4 = mybir.dt.float8_e4m3fn_x4
ALU = mybir.AluOpType
ACT = mybir.ActivationFunctionType

P = 128
PACK = 4
CH = 128
SCORE_SCALE = 0.0625


def tile_picked_candhinge_none_p_kernel(tc, x_words, x_scales, w1, gs, offs, cand, neg, out):
    nc = tc.nc
    with ExitStack() as ctx:
        lists = ctx.enter_context(tc.tile_pool(name="lists", bufs=1))
        sb = ctx.enter_context(tc.tile_pool(name="sb", bufs=1))
        ps = ctx.enter_context(tc.psum_pool(name="ps", bufs=1))

        offs_t = lists.tile([P, S // 16], U16, name="offs_t")
        cand_t = lists.tile([P, V // 16], U16, name="cand_t")
        neg_t = lists.tile([P, S // 16], U16, name="neg_t")

        xw = sb.tile([P, T], I32, name="xw", align_bytes=64)
        xs = sb.tile([P, T], U8, name="xs", align_bytes=64)
        gs_t = sb.tile([P, PACK], F32, name="gs_t")
        w_view = w1.rearrange("(p j) c -> p j c", j=PACK)
        w_parts = [(0, 1), (1, 3), (3, 4)]
        w_raw = [sb.tile([P, PACK, (c1 - c0) * CH], F32, name="w_raw%d" % c0, align_bytes=64) for c0, c1 in w_parts]

        def load_w(i):
            c0, c1 = w_parts[i]
            nc.sync.dma_start(out=w_raw[i][:], in_=w_view[:, :, c0 * CH : c1 * CH])

        nc.vector.memset(xs[:].bitcast(I32), 0)
        nc.gpsimd.dma_start(out=gs_t[:], in_=gs.rearrange("(p t) o -> p (t o)", t=PACK))
        nc.sync.dma_start(offs_t[:], offs)
        nc.sync.dma_start(cand_t[:], cand)
        load_w(0)
        for q in range(4):
            nc.sync.dma_start(out=xs[32 * q : 32 * q + 4, :].bitcast(I32), in_=x_scales[0, 4 * q : 4 * q + 4, :].bitcast(I32))
        load_w(1)
        load_w(2)
        nc.sync.dma_start(out=xw[:], in_=x_words[0].rearrange("p n t -> p (n t)").bitcast(I32))
        nc.sync.dma_start(neg_t[:], neg)

        tok_w = sb.tile([P, S], U32, name="tok_w", align_bytes=64)
        tok_s = sb.tile([P, S], U8, name="tok_s", align_bytes=64)
        cand_w = sb.tile([P, PACK, P], U32, name="cand_w", align_bytes=64)
        cand_s = sb.tile([P, PACK, P], U8, name="cand_s", align_bytes=64)
        nc.vector.tensor_copy(tok_s[:], xs[:].indirect(offs_t[:]))
        nc.vector.tensor_copy(cand_s[:].rearrange("p t m -> p m t"), xs[:].indirect(cand_t[:]))

        w_codes = sb.tile([P, PACK, P], U32, name="w_codes", align_bytes=64)
        w_scales = sb.tile([P, PACK, P], U8, name="w_scales", align_bytes=64)
        for half in range(2):
            w_bf = sb.tile([P, PACK, 64, PACK], BF16, name="w_bf%d" % half, align_bytes=64)
            for i in range(2):
                src = [w_raw[0][:], w_raw[1][:, :, 0:CH], w_raw[1][:, :, CH : 2 * CH], w_raw[2][:]][2 * half + i]
                cast = nc.vector.tensor_copy if 2 * half + i == 3 else nc.scalar.copy
                cast(
                    out=w_bf[:, :, 32 * i : 32 * i + 32, :].rearrange("p t m j -> p m t j"),
                    in_=src.rearrange("p j (m t) -> p m t j", t=PACK),
                )
            for t in range(PACK):
                nc.vector.quantize_mx(
                    out=w_codes[:, t, 64 * half : 64 * half + 64].bitcast(FP8X4),
                    scales=w_scales[:, t, 64 * half : 64 * half + 64],
                    in_=w_bf[:, t, :, :].rearrange("p m j -> p (m j)"),
                )

        for a, b in ((0, 128), (128, 256), (256, 512)):
            nc.vector.tensor_copy(tok_w[:, a:b], xw[:].bitcast(U32).indirect(offs_t[:, a // 16 : b // 16]))
        nc.vector.tensor_copy(cand_w[:].rearrange("p t m -> p m t"), xw[:].bitcast(U32).indirect(cand_t[:]))

        z_codes = sb.tile([P, S], U32, name="z_codes", align_bytes=64)
        z_scales = sb.tile([P, S], U8, name="z_scales", align_bytes=64)
        gs_b = gs_t[:].rearrange("p (o t) -> p o t", o=1).to_broadcast([P, CH, PACK])
        z_bf = []
        for c in range(4):
            cols = slice(c * CH, (c + 1) * CH)
            h_ps = ps.tile([P, PACK, CH], F32, name="h_ps%d" % c)
            for t in range(PACK):
                nc.tensor.matmul_mx(
                    out=h_ps[:, t, :],
                    lhsT=w_codes[:, t, :].bitcast(FP8X4), lhsT_scale=w_scales[:, t, :],
                    rhs=tok_w[:, cols].bitcast(FP8X4), rhs_scale=tok_s[:, cols],
                    start=True, stop=True,
                )
            zb = sb.tile([P, CH, PACK], BF16, name="z_bf%d" % c, align_bytes=64)
            z_bf.append((zb, h_ps))

        def scale_z(c):
            zb, h_ps = z_bf[c]
            nc.vector.scalar_tensor_tensor(
                out=zb[:], in0=h_ps[:].rearrange("p t n -> p n t"), scalar=0.0, in1=gs_b, op0=ALU.max, op1=ALU.mult
            )

        def quant_z(c):
            cols = slice(c * CH, (c + 1) * CH)
            nc.vector.quantize_mx(
                out=z_codes[:, cols].bitcast(FP8X4), scales=z_scales[:, cols], in_=z_bf[c][0][:].rearrange("p n t -> p (n t)")
            )

        def scale_z_aside(c):
            zb, h_ps = z_bf[c]
            pos = sb.tile([P, CH, PACK], F32, name="pos%d" % c, align_bytes=64)
            nc.scalar.activation(out=pos[:], in_=h_ps[:].rearrange("p t n -> p n t"), func=ACT.Relu)
            nc.gpsimd.tensor_tensor(out=zb[:], in0=pos[:], in1=gs_b, op=ALU.mult)

        s_ps = [[ps.tile([P, 2, 256], F32, name="s_ps%d_%d" % (u, g)) for g in range(2)] for u in range(2)]
        win = [sb.tile([P, S], F32, name="win%d" % t, align_bytes=64) for t in range(PACK)]

        def score(a, b, order):
            for t in order:
                nc.tensor.matmul_mx(
                    out=s_ps[a // 256][t // 2][:, t % 2, a % 256 : a % 256 + b - a],
                    lhsT=cand_w[:, t, :].bitcast(FP8X4), lhsT_scale=cand_s[:, t, :],
                    rhs=z_codes[:, a:b].bitcast(FP8X4), rhs_scale=z_scales[:, a:b],
                    start=True, stop=True,
                )

        def to_window(t, u, on_vector):
            dst = win[t][:, 256 * u : 256 * u + 256]
            src = s_ps[u][t // 2][:, t % 2, :]
            if on_vector:
                nc.vector.tensor_scalar(dst, src, SCORE_SCALE, 1.0, op0=ALU.mult, op1=ALU.add)
            else:
                nc.scalar.activation(out=dst, in_=src, func=ACT.Copy, scale=SCORE_SCALE, bias=1.0)

        scale_z_aside(0)
        scale_z(1)
        scale_z(2)
        quant_z(1)
        quant_z(0)
        score(0, 256, range(PACK))
        for t in range(PACK):
            to_window(t, 0, False)
        scale_z(3)
        quant_z(2)
        score(256, 384, range(PACK))
        quant_z(3)
        score(384, 512, range(PACK))

        out_v = out.rearrange("(p t) c -> t p c", t=PACK)
        got = {}
        diff = {}

        def fetch(t, u, on_vector):
            g = sb.tile([P, 256], F32, name="got%d_%d" % (t, u), align_bytes=64)
            got[(t, u)] = g
            src = win[t][:].indirect(neg_t[:, 16 * u : 16 * u + 16])
            if on_vector:
                nc.vector.tensor_copy(g[:], src)
            else:
                nc.scalar.activation(out=g[:], in_=src, func=ACT.Copy)

        def subtract(t, u):
            d = sb.tile([P, 256], F32, name="diff%d_%d" % (t, u), align_bytes=64)
            nc.vector.scalar_tensor_tensor(
                out=d[:], in0=s_ps[u][t // 2][:, t % 2, :], scalar=-SCORE_SCALE, in1=got[(t, u)][:], op0=ALU.mult, op1=ALU.add
            )
            diff[(t, u)] = d

        def finish(t, u, on_vector):
            d = diff[(t, u)]
            r = sb.tile([P, 256], F32, name="res%d_%d" % (t, u), align_bytes=64)
            if not on_vector:
                nc.scalar.activation(out=r[:], in_=d[:], func=ACT.Relu)
            else:
                nc.vector.tensor_scalar(r[:], d[:], 0.0, None, op0=ALU.max)
            nc.sync.dma_start(out=out_v[t, :, 256 * u : 256 * u + 256], in_=r[:])

        to_window(0, 1, False)
        to_window(3, 1, True)
        to_window(2, 1, True)
        fetch(0, 0, False)
        fetch(3, 0, True)
        fetch(0, 1, False)
        to_window(1, 1, False)
        subtract(0, 0)
        subtract(3, 0)
        finish(0, 0, True)
        fetch(3, 1, True)
        finish(3, 0, True)
        fetch(1, 0, False)
        fetch(1, 1, False)
        fetch(2, 0, False)
        fetch(2, 1, False)
        subtract(0, 1)
        subtract(3, 1)
        finish(0, 1, True)
        subtract(1, 0)
        finish(3, 1, True)
        subtract(1, 1)
        finish(1, 0, True)
        subtract(2, 0)
        finish(1, 1, False)
        subtract(2, 1)
        finish(2, 0, False)
        finish(2, 1, True)
